import numpy as np
import ml_dtypes


def mxq(x, axis, fmt="e4m3"):
    dtype, down = {"e4m3": (ml_dtypes.float8_e4m3fn, 7), "e5m2": (ml_dtypes.float8_e5m2, 14)}[fmt]
    v = np.moveaxis(np.asarray(x, np.float32).astype(ml_dtypes.bfloat16).astype(np.float64), axis, -1)
    blocks = v.reshape(v.shape[:-1] + (-1, 32))
    amax = np.abs(blocks).max(-1, keepdims=True)
    byte = np.maximum(np.where(amax > 0, np.frexp(amax)[1] - 1 + 127, 0) - down, 1)
    scale = np.exp2(byte - 127.0)
    codes = (blocks / scale).astype(np.float32).astype(dtype).astype(np.float64)
    return np.moveaxis((codes * scale).reshape(v.shape), -1, axis)


WIDE = False


def mx_kscale(k):
    if not WIDE:
        return np.ones(k)
    levels = np.array([10, -10, 5, -5, 0])
    if k % 512:
        return np.exp2(np.random.permutation(np.resize(levels, k // 32))).repeat(32)
    a = np.empty((k // 512, 16))
    for p in range(k // 512):
        a[p, :8] = np.random.permutation(np.resize(levels, 8))
        for g in range(8):
            far = levels[np.abs(levels - a[p, g]) >= 10]
            a[p, g + 8] = far[np.random.randint(len(far))]
    return np.exp2(a.ravel()).repeat(32)


def f64(x):
    return np.asarray(x).astype(np.float64)


def striped(idx):
    return np.tile(idx.reshape(-1, 16).T, (8, 1)).astype(np.uint16)


def unstriped(offs):
    return offs[:16].T.reshape(-1).astype(np.int64)


def pack_weight(w):
    k, n = w.shape
    w = f64(np.asarray(w, np.float32).astype(ml_dtypes.bfloat16)).reshape(k // 32, 32, n)
    amax = np.abs(w).max(1)
    byte = np.clip(np.where(amax > 0, np.frexp(amax)[1] - 1 + 127 - 7, 1), 1, 254)
    scaled = (w * np.exp2(127.0 - byte)[:, None, :]).reshape(k, n).astype(np.float32)
    words = np.ascontiguousarray(scaled.reshape(k // 512, 128, 4, n).transpose(0, 1, 3, 2)).astype(ml_dtypes.float8_e4m3fn).view(np.uint8)
    return words, np.ascontiguousarray(byte.astype(np.uint8).reshape(k // 512, 16, n))


def unpack_weight(words, scales):
    g, p, n, _ = words.shape
    vals = np.ascontiguousarray(words).view(ml_dtypes.float8_e4m3fn).astype(np.float64) * np.repeat(np.exp2(scales.astype(np.float64) - 127.0), 8, axis=1)[..., None]
    return vals.transpose(0, 1, 3, 2).reshape(g * 512, n)


K, T, E, C, N = 1536, 2048, 8, 128, 256


def by_expert(wq, xq):
    return np.concatenate([wq[e].T @ xq[:, e * C:(e + 1) * C] for e in range(E)], axis=1)


def setup_inputs():
    n = np.random.standard_normal
    s = mx_kscale(K)[:, None]
    packed = [pack_weight(m) for m in n((E, K, N)) / np.sqrt(K) / s[None]]
    return {
        "xT": (n((K, T)) * s).astype(np.float32),
        "w_words": np.stack([m[0] for m in packed]),
        "w_scales": np.stack([m[1] for m in packed]),
        "gate": np.tile(np.random.uniform(0.2, 1.0, E * C), (N, 1)).astype(np.float32),
        "offs": striped(np.random.permutation(T)[:E * C]),
    }


def reference(xT, w_words, w_scales, gate, offs):
    idx = unstriped(offs)
    xq = mxq(f64(xT)[:, idx], 0, "e4m3")
    w = np.stack([unpack_weight(w_words[e], w_scales[e]) for e in range(E)])
    y = by_expert(w, xq)
    out = np.zeros((N, T))
    out[:, idx] = f64(gate) * y
    return out

@@ -1,0 +1,117 @@
+from contextlib import ExitStack
+
+import concourse.mybir as mybir
+
+K, T, E, C, N = 1536, 2048, 8, 128, 256
+FLOPS = 2 * K * E * C * N
+
+F32 = mybir.dt.float32
+BF16 = mybir.dt.bfloat16
+I32 = mybir.dt.int32
+U32 = mybir.dt.uint32
+U16 = mybir.dt.uint16
+U8 = mybir.dt.uint8
+FP8X4 = mybir.dt.float8_e4m3fn_x4
+MULT = mybir.AluOpType.mult
+
+P = 128
+PASSES = 3
+SLOTS = E * C
+HALF = SLOTS // 2
+EVEN = ((0, 512, 320), (512, 512, 320), (1024, 512, 320), (1536, 512, 320))
+LAST = ((0, 512, 320), (512, 512, 320), (1024, 512, 304), (1536, 256, 128), (1792, 256, 112))
+
+
+def interleave(copy, dst, src):
+    copy(out=dst.rearrange("p (c i) t -> p c t i", i=4), in_=src.rearrange("p t (c i) -> p c t i", i=4))
+
+
+def tile_routed_moe_kernel(tc, xT, w_words, w_scales, gate, offs, out):
+    nc = tc.nc
+    x_view = xT.rearrange("(g p t) n -> g p t n", p=P, t=4)
+    with ExitStack() as ctx:
+        keep = ctx.enter_context(tc.tile_pool(name="keep", bufs=1))
+        stage = ctx.enter_context(tc.tile_pool(name="stage", bufs=4))
+        psum = ctx.enter_context(tc.psum_pool(name="psum", bufs=1))
+
+        offsets = keep.tile([P, SLOTS // 16], U16, name="offsets")
+        planes = keep.tile([P, T], U8, name="planes", align_bytes=64)
+        w_planes = keep.tile([P, E * PASSES, N], U8, name="w_planes", align_bytes=64)
+        windows = [keep.tile([P, T], F32, name=f"window{b}") for b in range(2)]
+        nc.gpsimd.memset(planes[:], 0)
+        nc.vector.memset(w_planes[:].rearrange("p c n -> p (c n)").bitcast(I32), 0)
+        for b in range(2):
+            nc.vector.memset(windows[b][:], 0.0)
+
+        chunks = []
+        for a in range(PASSES):
+            for t0, width, share in (LAST if a == PASSES - 1 else EVEN):
+                raw = keep.tile([P, 4, width], F32, name=f"raw{a}_{t0}")
+                nc.sync.dma_start(raw[:], x_view[a, :, :, t0 : t0 + width])
+                chunks.append((a, t0, width, share, raw))
+                if len(chunks) == 1:
+                    nc.sync.dma_start(offsets[:], offs)
+        w_tiles = []
+        gate_tiles = []
+        for pair in range(E // 2):
+            w = keep.tile([P, 2 * PASSES, N], U32, name=f"w{pair}", align_bytes=64)
+            src = w_words[2 * pair : 2 * pair + 2].rearrange("e a p n r -> p (e a) (n r)")
+            nc.sync.dma_start(w[:].bitcast(I32), src.bitcast(I32))
+            w_tiles.append(w)
+            if pair == 0:
+                for q in range(4):
+                    src = w_scales.rearrange("e a q n -> q (e a) n")[4 * q : 4 * q + 4]
+                    nc.sync.dma_start(w_planes[32 * q : 32 * q + 4].bitcast(I32), src.bitcast(I32))
+            if pair % 2 == 1:
+                g = keep.tile([P, SLOTS], F32, name=f"gate{pair // 2}")
+                b = pair // 2
+                nc.sync.dma_start(g[:], gate[b * P : (b + 1) * P, :])
+                gate_tiles.append(g)
+
+        codes = [keep.tile([P, T], U32, name=f"codes{a}", align_bytes=64) for a in range(PASSES)]
+        words = [[keep.tile([P, HALF], U32, name=f"words{a}_{h}", align_bytes=64) for h in range(2)] for a in range(PASSES)]
+        slot_planes = [keep.tile([P, HALF], U8, name=f"slot_planes{h}", align_bytes=64) for h in range(2)]
+
+        def gather(h, dst, window):
+            nc.vector.tensor_copy(dst[:], window[:].indirect(offsets[:, h * HALF // 16 : (h + 1) * HALF // 16]))
+
+        for a, t0, width, share, raw in chunks:
+            grouped = stage.tile([P, 512, 4], BF16, name="grouped", align_bytes=64)
+            interleave(nc.scalar.copy, grouped[:, 0:share], raw[:, :, 0:share])
+            interleave(nc.vector.tensor_copy, grouped[:, share:width], raw[:, :, share:width])
+            nc.vector.quantize_mx(
+                out=codes[a][:, t0 : t0 + width].bitcast(FP8X4),
+                scales=planes[4 * a : P, t0 : t0 + width],
+                in_=grouped[:, 0:width].rearrange("p w t -> p (w t)"),
+            )
+            if t0 + width == T and a < PASSES - 1:
+                for h in range(2):
+                    gather(h, words[a][h], codes[a])
+        for h in range(2):
+            gather(h, words[PASSES - 1][h], codes[PASSES - 1])
+            gather(h, slot_planes[h], planes)
+
+        sums = {}
+        for h in range(2):
+            for b in range(2):
+                bank = psum.tile([P, HALF], F32, name=f"sums{h}_{b}")
+                sums[(h, b)] = bank
+                for i in range(E // 2):
+                    e = h * E // 2 + i
+                    cols = slice(i * C, (i + 1) * C)
+                    for a in range(PASSES):
+                        nc.tensor.matmul_mx(
+                            out=bank[:, cols],
+                            lhsT=w_tiles[e // 2][:, e % 2 * PASSES + a, b * P : (b + 1) * P].bitcast(FP8X4),
+                            lhsT_scale=w_planes[:, e * PASSES + a, b * P : (b + 1) * P],
+                            rhs=words[a][h][:, cols].bitcast(FP8X4),
+                            rhs_scale=slot_planes[h][4 * a : P, cols],
+                            start=(a == 0),
+                            stop=(a == PASSES - 1),
+                        )
+        for b in range(2):
+            for h in range(2):
+                y = keep.tile([P, HALF], F32, name=f"y{b}_{h}")
+                nc.vector.tensor_tensor(y[:], sums[(h, b)][:], gate_tiles[b][:, h * HALF : (h + 1) * HALF], MULT)
+                nc.vector.tensor_copy(windows[b][:].indirect(offsets[:, h * HALF // 16 : (h + 1) * HALF // 16]), y[:])
+            nc.sync.dma_start(out[b * P : (b + 1) * P, :], windows[b][:])

@@ -18,8 +18,10 @@ P = 128
 PASSES = 3
 SLOTS = E * C
 HALF = SLOTS // 2
-EVEN = ((0, 512, 320), (512, 512, 320), (1024, 512, 320), (1536, 512, 320))
-LAST = ((0, 512, 320), (512, 512, 320), (1024, 512, 304), (1536, 256, 128), (1792, 256, 112))
+LOADS = ((0, 1024), (1024, 1024))
+LAST_LOADS = ((0, 1024), (1024, 768), (1792, 256))
+SHARE = {512: 384, 256: 128}
+UNITS = ((0, 0, 256), (1, 0, 256), (0, 256, 256), (1, 256, 256), (0, 512, 512), (1, 512, 512))
 
 
 def interleave(copy, dst, src):
@@ -45,37 +47,47 @@ def tile_routed_moe_kernel(tc, xT, w_words, w_scales, gate, offs, out):
 
         chunks = []
         for a in range(PASSES):
-            for t0, width, share in (LAST if a == PASSES - 1 else EVEN):
+            for t0, width in (LAST_LOADS if a == PASSES - 1 else LOADS):
                 raw = keep.tile([P, 4, width], F32, name=f"raw{a}_{t0}")
                 nc.sync.dma_start(raw[:], x_view[a, :, :, t0 : t0 + width])
-                chunks.append((a, t0, width, share, raw))
-                if len(chunks) == 1:
+                done = 0
+                while done < width:
+                    w = min(512, width - done)
+                    chunks.append((a, t0 + done, w, raw[:, :, done : done + w]))
+                    done += w
+                if a == 0 and t0 == 0:
                     nc.sync.dma_start(offsets[:], offs)
-        w_tiles = []
-        gate_tiles = []
-        for pair in range(E // 2):
-            w = keep.tile([P, 2 * PASSES, N], U32, name=f"w{pair}", align_bytes=64)
+        w_tiles = [keep.tile([P, 2 * PASSES, N], U32, name=f"w{pair}", align_bytes=64) for pair in range(E // 2)]
+        gates = [keep.tile([P, SLOTS], F32, name=f"gate{b}") for b in range(2)]
+
+        def load_weights(pair):
             src = w_words[2 * pair : 2 * pair + 2].rearrange("e a p n r -> p (e a) (n r)")
-            nc.sync.dma_start(w[:].bitcast(I32), src.bitcast(I32))
-            w_tiles.append(w)
-            if pair == 0:
-                for q in range(4):
-                    src = w_scales.rearrange("e a q n -> q (e a) n")[4 * q : 4 * q + 4]
-                    nc.sync.dma_start(w_planes[32 * q : 32 * q + 4].bitcast(I32), src.bitcast(I32))
-            if pair % 2 == 1:
-                g = keep.tile([P, SLOTS], F32, name=f"gate{pair // 2}")
-                b = pair // 2
-                nc.sync.dma_start(g[:], gate[b * P : (b + 1) * P, :])
-                gate_tiles.append(g)
+            nc.sync.dma_start(w_tiles[pair][:].bitcast(I32), src.bitcast(I32))
+
+        def load_gates(h):
+            for b in range(2):
+                cols = slice(h * HALF, (h + 1) * HALF)
+                nc.sync.dma_start(gates[b][:, cols], gate[b * P : (b + 1) * P, cols])
+
+        load_weights(0)
+        for q in range(4):
+            src = w_scales.rearrange("e a q n -> q (e a) n")[4 * q : 4 * q + 4]
+            nc.sync.dma_start(w_planes[32 * q : 32 * q + 4].bitcast(I32), src.bitcast(I32))
+        load_gates(0)
+        load_weights(1)
+        load_weights(2)
+        load_weights(3)
+        load_gates(1)
 
         codes = [keep.tile([P, T], U32, name=f"codes{a}", align_bytes=64) for a in range(PASSES)]
-        words = [[keep.tile([P, HALF], U32, name=f"words{a}_{h}", align_bytes=64) for h in range(2)] for a in range(PASSES)]
-        slot_planes = [keep.tile([P, HALF], U8, name=f"slot_planes{h}", align_bytes=64) for h in range(2)]
+        words = [keep.tile([P, SLOTS], U32, name=f"words{a}", align_bytes=64) for a in range(PASSES)]
+        slot_planes = keep.tile([P, SLOTS], U8, name="slot_planes", align_bytes=64)
 
-        def gather(h, dst, window):
-            nc.vector.tensor_copy(dst[:], window[:].indirect(offsets[:, h * HALF // 16 : (h + 1) * HALF // 16]))
+        def gather(dst, window, s0, n):
+            nc.vector.tensor_copy(dst[:, s0 : s0 + n], window[:].indirect(offsets[:, s0 // 16 : (s0 + n) // 16]))
 
-        for a, t0, width, share, raw in chunks:
+        for a, t0, width, raw in chunks:
+            share = SHARE[width]
             grouped = stage.tile([P, 512, 4], BF16, name="grouped", align_bytes=64)
             interleave(nc.scalar.copy, grouped[:, 0:share], raw[:, :, 0:share])
             interleave(nc.vector.tensor_copy, grouped[:, share:width], raw[:, :, share:width])
@@ -85,33 +97,29 @@ def tile_routed_moe_kernel(tc, xT, w_words, w_scales, gate, offs, out):
                 in_=grouped[:, 0:width].rearrange("p w t -> p (w t)"),
             )
             if t0 + width == T and a < PASSES - 1:
-                for h in range(2):
-                    gather(h, words[a][h], codes[a])
+                gather(words[a], codes[a], 0, SLOTS)
         for h in range(2):
-            gather(h, words[PASSES - 1][h], codes[PASSES - 1])
-            gather(h, slot_planes[h], planes)
+            gather(words[PASSES - 1], codes[PASSES - 1], h * HALF, HALF)
+            gather(slot_planes, planes, h * HALF, HALF)
 
-        sums = {}
-        for h in range(2):
-            for b in range(2):
-                bank = psum.tile([P, HALF], F32, name=f"sums{h}_{b}")
-                sums[(h, b)] = bank
-                for i in range(E // 2):
-                    e = h * E // 2 + i
-                    cols = slice(i * C, (i + 1) * C)
-                    for a in range(PASSES):
-                        nc.tensor.matmul_mx(
-                            out=bank[:, cols],
-                            lhsT=w_tiles[e // 2][:, e % 2 * PASSES + a, b * P : (b + 1) * P].bitcast(FP8X4),
-                            lhsT_scale=w_planes[:, e * PASSES + a, b * P : (b + 1) * P],
-                            rhs=words[a][h][:, cols].bitcast(FP8X4),
-                            rhs_scale=slot_planes[h][4 * a : P, cols],
-                            start=(a == 0),
-                            stop=(a == PASSES - 1),
-                        )
-        for b in range(2):
-            for h in range(2):
-                y = keep.tile([P, HALF], F32, name=f"y{b}_{h}")
-                nc.vector.tensor_tensor(y[:], sums[(h, b)][:], gate_tiles[b][:, h * HALF : (h + 1) * HALF], MULT)
-                nc.vector.tensor_copy(windows[b][:].indirect(offsets[:, h * HALF // 16 : (h + 1) * HALF // 16]), y[:])
-            nc.sync.dma_start(out[b * P : (b + 1) * P, :], windows[b][:])
+        for u, (b, s0, n) in enumerate(UNITS):
+            bank = psum.tile([P, n], F32, name=f"sums{u}")
+            for e in range(s0 // C, (s0 + n) // C):
+                cols = slice(e * C, (e + 1) * C)
+                for a in range(PASSES):
+                    nc.tensor.matmul_mx(
+                        out=bank[:, e * C - s0 : (e + 1) * C - s0],
+                        lhsT=w_tiles[e // 2][:, e % 2 * PASSES + a, b * P : (b + 1) * P].bitcast(FP8X4),
+                        lhsT_scale=w_planes[:, e * PASSES + a, b * P : (b + 1) * P],
+                        rhs=words[a][:, cols].bitcast(FP8X4),
+                        rhs_scale=slot_planes[4 * a : P, cols],
+                        start=(a == 0),
+                        stop=(a == PASSES - 1),
+                    )
+            y = keep.tile([P, n], F32, name=f"y{u}")
+            nc.scalar.copy(y[:], bank[:])
+            nc.vector.tensor_tensor(
+                windows[b][:].indirect(offsets[:, s0 // 16 : (s0 + n) // 16]), y[:], gates[b][:, s0 : s0 + n], MULT
+            )
+            if s0 + n == SLOTS:
+                nc.sync.dma_start(out[b * P : (b + 1) * P, :], windows[b][:])

@@ -18,9 +18,8 @@ P = 128
 PASSES = 3
 SLOTS = E * C
 HALF = SLOTS // 2
-LOADS = ((0, 1024), (1024, 1024))
-LAST_LOADS = ((0, 1024), (1024, 768), (1792, 256))
-SHARE = {512: 384, 256: 128}
+LOADS = (((0, 1024), (1024, 1024)), ((0, 1024), (1024, 1024)), ((0, 1280), (1280, 512), (1792, 256)))
+SHARES = ({512: 400}, {512: 384}, {512: 288, 256: 144})
 UNITS = ((0, 0, 256), (1, 0, 256), (0, 256, 256), (1, 256, 256), (0, 512, 512), (1, 512, 512))
 
 
@@ -47,7 +46,7 @@ def tile_routed_moe_kernel(tc, xT, w_words, w_scales, gate, offs, out):
 
         chunks = []
         for a in range(PASSES):
-            for t0, width in (LAST_LOADS if a == PASSES - 1 else LOADS):
+            for t0, width in LOADS[a]:
                 raw = keep.tile([P, 4, width], F32, name=f"raw{a}_{t0}")
                 nc.sync.dma_start(raw[:], x_view[a, :, :, t0 : t0 + width])
                 done = 0
@@ -69,10 +68,10 @@ def tile_routed_moe_kernel(tc, xT, w_words, w_scales, gate, offs, out):
                 cols = slice(h * HALF, (h + 1) * HALF)
                 nc.sync.dma_start(gates[b][:, cols], gate[b * P : (b + 1) * P, cols])
 
-        load_weights(0)
         for q in range(4):
             src = w_scales.rearrange("e a q n -> q (e a) n")[4 * q : 4 * q + 4]
             nc.sync.dma_start(w_planes[32 * q : 32 * q + 4].bitcast(I32), src.bitcast(I32))
+        load_weights(0)
         load_gates(0)
         load_weights(1)
         load_weights(2)
@@ -87,7 +86,7 @@ def tile_routed_moe_kernel(tc, xT, w_words, w_scales, gate, offs, out):
             nc.vector.tensor_copy(dst[:, s0 : s0 + n], window[:].indirect(offsets[:, s0 // 16 : (s0 + n) // 16]))
 
         for a, t0, width, raw in chunks:
-            share = SHARE[width]
+            share = SHARES[a][width]
             grouped = stage.tile([P, 512, 4], BF16, name="grouped", align_bytes=64)
             interleave(nc.scalar.copy, grouped[:, 0:share], raw[:, :, 0:share])
             interleave(nc.vector.tensor_copy, grouped[:, share:width], raw[:, :, share:width])

from contextlib import ExitStack

import concourse.mybir as mybir

K, T, E, C, N = 1536, 2048, 8, 128, 256
FLOPS = 2 * K * E * C * N

F32 = mybir.dt.float32
BF16 = mybir.dt.bfloat16
I32 = mybir.dt.int32
U32 = mybir.dt.uint32
U16 = mybir.dt.uint16
U8 = mybir.dt.uint8
FP8X4 = mybir.dt.float8_e4m3fn_x4
MULT = mybir.AluOpType.mult

P = 128
PASSES = 3
SLOTS = E * C
HALF = SLOTS // 2
LOADS = (((0, 1024), (1024, 1024)), ((0, 1024), (1024, 1024)), ((0, 1280), (1280, 512), (1792, 256)))
SHARES = ({512: 400}, {512: 384}, {512: 288, 256: 144})
UNITS = ((0, 0, 256), (1, 0, 256), (0, 256, 256), (1, 256, 256), (0, 512, 512), (1, 512, 512))


def interleave(copy, dst, src):
    copy(out=dst.rearrange("p (c i) t -> p c t i", i=4), in_=src.rearrange("p t (c i) -> p c t i", i=4))


def tile_routed_moe_kernel(tc, xT, w_words, w_scales, gate, offs, out):
    nc = tc.nc
    x_view = xT.rearrange("(g p t) n -> g p t n", p=P, t=4)
    with ExitStack() as ctx:
        keep = ctx.enter_context(tc.tile_pool(name="keep", bufs=1))
        stage = ctx.enter_context(tc.tile_pool(name="stage", bufs=4))
        psum = ctx.enter_context(tc.psum_pool(name="psum", bufs=1))

        offsets = keep.tile([P, SLOTS // 16], U16, name="offsets")
        planes = keep.tile([P, T], U8, name="planes", align_bytes=64)
        w_planes = keep.tile([P, E * PASSES, N], U8, name="w_planes", align_bytes=64)
        windows = [keep.tile([P, T], F32, name=f"window{b}") for b in range(2)]
        nc.gpsimd.memset(planes[:], 0)
        nc.vector.memset(w_planes[:].rearrange("p c n -> p (c n)").bitcast(I32), 0)
        for b in range(2):
            nc.vector.memset(windows[b][:], 0.0)

        chunks = []
        for a in range(PASSES):
            for t0, width in LOADS[a]:
                raw = keep.tile([P, 4, width], F32, name=f"raw{a}_{t0}")
                nc.sync.dma_start(raw[:], x_view[a, :, :, t0 : t0 + width])
                done = 0
                while done < width:
                    w = min(512, width - done)
                    chunks.append((a, t0 + done, w, raw[:, :, done : done + w]))
                    done += w
                if a == 0 and t0 == 0:
                    nc.sync.dma_start(offsets[:], offs)
        w_tiles = [keep.tile([P, 2 * PASSES, N], U32, name=f"w{pair}", align_bytes=64) for pair in range(E // 2)]
        gates = [keep.tile([P, SLOTS], F32, name=f"gate{b}") for b in range(2)]

        def load_weights(pair):
            src = w_words[2 * pair : 2 * pair + 2].rearrange("e a p n r -> p (e a) (n r)")
            nc.sync.dma_start(w_tiles[pair][:].bitcast(I32), src.bitcast(I32))

        def load_gates(h):
            for b in range(2):
                cols = slice(h * HALF, (h + 1) * HALF)
                nc.sync.dma_start(gates[b][:, cols], gate[b * P : (b + 1) * P, cols])

        for q in range(4):
            src = w_scales.rearrange("e a q n -> q (e a) n")[4 * q : 4 * q + 4]
            nc.sync.dma_start(w_planes[32 * q : 32 * q + 4].bitcast(I32), src.bitcast(I32))
        load_weights(0)
        load_gates(0)
        load_weights(1)
        load_weights(2)
        load_weights(3)
        load_gates(1)

        codes = [keep.tile([P, T], U32, name=f"codes{a}", align_bytes=64) for a in range(PASSES)]
        words = [keep.tile([P, SLOTS], U32, name=f"words{a}", align_bytes=64) for a in range(PASSES)]
        slot_planes = keep.tile([P, SLOTS], U8, name="slot_planes", align_bytes=64)

        def gather(dst, window, s0, n):
            nc.vector.tensor_copy(dst[:, s0 : s0 + n], window[:].indirect(offsets[:, s0 // 16 : (s0 + n) // 16]))

        for a, t0, width, raw in chunks:
            share = SHARES[a][width]
            grouped = stage.tile([P, 512, 4], BF16, name="grouped", align_bytes=64)
            interleave(nc.scalar.copy, grouped[:, 0:share], raw[:, :, 0:share])
            interleave(nc.vector.tensor_copy, grouped[:, share:width], raw[:, :, share:width])
            nc.vector.quantize_mx(
                out=codes[a][:, t0 : t0 + width].bitcast(FP8X4),
                scales=planes[4 * a : P, t0 : t0 + width],
                in_=grouped[:, 0:width].rearrange("p w t -> p (w t)"),
            )
            if t0 + width == T and a < PASSES - 1:
                gather(words[a], codes[a], 0, SLOTS)
        for h in range(2):
            gather(words[PASSES - 1], codes[PASSES - 1], h * HALF, HALF)
            gather(slot_planes, planes, h * HALF, HALF)

        for u, (b, s0, n) in enumerate(UNITS):
            bank = psum.tile([P, n], F32, name=f"sums{u}")
            for e in range(s0 // C, (s0 + n) // C):
                cols = slice(e * C, (e + 1) * C)
                for a in range(PASSES):
                    nc.tensor.matmul_mx(
                        out=bank[:, e * C - s0 : (e + 1) * C - s0],
                        lhsT=w_tiles[e // 2][:, e % 2 * PASSES + a, b * P : (b + 1) * P].bitcast(FP8X4),
                        lhsT_scale=w_planes[:, e * PASSES + a, b * P : (b + 1) * P],
                        rhs=words[a][:, cols].bitcast(FP8X4),
                        rhs_scale=slot_planes[4 * a : P, cols],
                        start=(a == 0),
                        stop=(a == PASSES - 1),
                    )
            y = keep.tile([P, n], F32, name=f"y{u}")
            nc.scalar.copy(y[:], bank[:])
            nc.vector.tensor_tensor(
                windows[b][:].indirect(offsets[:, s0 // 16 : (s0 + n) // 16]), y[:], gates[b][:, s0 : s0 + n], MULT
            )
            if s0 + n == SLOTS:
                nc.sync.dma_start(out[b * P : (b + 1) * P, :], windows[b][:])
